import numpy as np
import ml_dtypes


def mxq(x, axis, fmt="e4m3"):
    dtype, down = {"e4m3": (ml_dtypes.float8_e4m3fn, 7), "e5m2": (ml_dtypes.float8_e5m2, 14)}[fmt]
    v = np.moveaxis(np.asarray(x, np.float32).astype(ml_dtypes.bfloat16).astype(np.float64), axis, -1)
    blocks = v.reshape(v.shape[:-1] + (-1, 32))
    amax = np.abs(blocks).max(-1, keepdims=True)
    byte = np.maximum(np.where(amax > 0, np.frexp(amax)[1] - 1 + 127, 0) - down, 1)
    scale = np.exp2(byte - 127.0)
    codes = (blocks / scale).astype(np.float32).astype(dtype).astype(np.float64)
    return np.moveaxis((codes * scale).reshape(v.shape), -1, axis)


WIDE = False


def mx_kscale(k):
    if not WIDE:
        return np.ones(k)
    levels = np.array([10, -10, 5, -5, 0])
    if k % 512:
        return np.exp2(np.random.permutation(np.resize(levels, k // 32))).repeat(32)
    a = np.empty((k // 512, 16))
    for p in range(k // 512):
        a[p, :8] = np.random.permutation(np.resize(levels, 8))
        for g in range(8):
            far = levels[np.abs(levels - a[p, g]) >= 10]
            a[p, g + 8] = far[np.random.randint(len(far))]
    return np.exp2(a.ravel()).repeat(32)


BF16 = ml_dtypes.bfloat16


def bf(x):
    return np.asarray(x, np.float32).astype(BF16)


def f64(x):
    return np.asarray(x).astype(np.float64)

def planes(Y):
    n, m = Y.shape
    b = f64(bf(Y)).reshape(n // 32, 32, m)
    amax = np.abs(b).max(1)
    byte = np.clip(np.where(amax > 0, np.frexp(amax)[1] - 1 + 127 - 7, 1), 1, 254)
    codes = (b * np.exp2(127.0 - byte)[:, None, :]).reshape(n, m).astype(np.float32).astype(ml_dtypes.float8_e4m3fn).view(np.uint8)
    words = codes.reshape(n // 512, 128, 4, m).transpose(0, 1, 3, 2)
    return np.ascontiguousarray(words), np.ascontiguousarray(byte.astype(np.uint8).reshape(n // 512, 16, m))


NODES, CLUSTERS, FEATS = 4096, 512, 1024

OWN_LOGIT = 7.0
NODE_NOISE = 0.7


def setup_inputs():
    rnd = np.random.randn
    s = mx_kscale(NODES)
    home = np.random.permutation(NODES) % CLUSTERS
    logits = rnd(NODES, CLUSTERS) + 0.5 * rnd(CLUSTERS)[None, :]
    logits[np.arange(NODES), home] += OWN_LOGIT
    e = np.exp(logits - logits.max(axis=1, keepdims=True))
    soft = e / e.sum(axis=1, keepdims=True)
    x = rnd(CLUSTERS, FEATS)[home] + NODE_NOISE * rnd(NODES, FEATS)
    return {
        "assign": bf(soft * s[:, None]),
        "x": bf(x / s[:, None]),
        "sizes": bf(soft.sum(axis=0)),
        "shift": bf(0.3 * rnd(FEATS)),
        "gain": bf(np.exp(0.7 * rnd(FEATS))),
    }


def reference(assign, x, sizes, shift, gain):
    total = mxq(f64(assign), 0, "e4m3").T @ mxq(f64(x), 0, "e4m3")
    pooled = total / f64(sizes)[:, None]
    y = (pooled + f64(shift)[None, :]) * f64(gain)[None, :]
    Y = y.T
    words, scales = planes(Y)
    return y, words, scales

@@ -1,0 +1,267 @@
+from contextlib import ExitStack
+
+import concourse.mybir as mybir
+from concourse.masks import make_identity
+
+NODES, CLUSTERS, FEATS = 4096, 512, 1024
+FLOPS = 2 * NODES * CLUSTERS * FEATS
+
+F32 = mybir.dt.float32
+BF16 = mybir.dt.bfloat16
+I32 = mybir.dt.int32
+U32 = mybir.dt.uint32
+U8 = mybir.dt.uint8
+FP8X4 = mybir.dt.float8_e4m3fn_x4
+ALU = mybir.AluOpType
+
+P = 128
+PACK = 4
+K_PASS = P * PACK
+PASSES = NODES // K_PASS
+WIDTH = 512
+HALVES = FEATS // WIDTH
+C_TILES = CLUSTERS // P
+RUN = 4
+SCALAR_COLS = 256
+SCALAR_COLS_EPILOGUE = 320
+SIZE_ROW = 0
+SHIFT_ROW = SIZE_ROW + C_TILES
+GAIN_ROW = SHIFT_ROW + FEATS // P
+VECTOR_ROWS = GAIN_ROW + FEATS // P
+
+
+def tile_cluster_mean_pool_g1_kernel(tc, assign, x, sizes, shift, gain, out_0, out_1, out_2):
+    nc = tc.nc
+
+    with ExitStack() as ctx:
+        keep = ctx.enter_context(tc.tile_pool(name="keep", bufs=1))
+        stream = ctx.enter_context(tc.tile_pool(name="stream", bufs=4))
+        psum = ctx.enter_context(tc.psum_pool(name="psum", bufs=1))
+        ctx.enter_context(tc.manual_schedule())
+
+        def bank(index, shape, dtype):
+            return psum.tile(shape, dtype, name="bank%d" % index, tag="bank%d" % index)
+
+        chunks = []
+        for i in range(PASSES):
+            chunks.append(("x", i, 0))
+            chunks.append(("assign", i, 0))
+        for i in range(PASSES):
+            chunks.append(("x", i, 1))
+
+        rows = keep.tile([P, P], BF16, name="rows")
+        nc.vector.memset(rows[:], 0.0)
+        nc.scalar.dma_start(out=rows[SIZE_ROW:SHIFT_ROW, :], in_=sizes.rearrange("(j p) -> j p", p=P))
+        nc.scalar.dma_start(out=rows[SHIFT_ROW:GAIN_ROW, :], in_=shift.rearrange("(j p) -> j p", p=P))
+        nc.scalar.dma_start(out=rows[GAIN_ROW:VECTOR_ROWS, :], in_=gain.rearrange("(j p) -> j p", p=P))
+        ident_bf16 = keep.tile([P, P], BF16, name="ident_bf16")
+        ident_f32 = keep.tile([P, P], F32, name="ident_f32")
+        make_identity(nc, ident_bf16[:])
+        make_identity(nc, ident_f32[:])
+
+        raw = []
+        for n, (kind, i, half) in enumerate(chunks):
+            source = assign if kind == "assign" else x
+            block = source[i * K_PASS:(i + 1) * K_PASS, half * WIDTH:(half + 1) * WIDTH]
+            block = block.rearrange("(p j) w -> p j w", j=PACK)
+            if n == 0:
+                parts = []
+                for lo, hi in ((SCALAR_COLS, WIDTH), (0, SCALAR_COLS)):
+                    loaded = keep.tile([P, PACK, hi - lo], BF16, name="raw0_%d" % lo)
+                    nc.sync.dma_start(out=loaded[:], in_=block[:, :, lo:hi])
+                    parts.append(loaded)
+                raw.append(parts)
+            else:
+                loaded = keep.tile([P, PACK, WIDTH], BF16, name="raw%d" % n)
+                nc.sync.dma_start(out=loaded[:], in_=block)
+                raw.append(loaded)
+
+        grouped = {}
+        codes = {}
+        scales = {}
+
+        def interleave(n, scalar_cols):
+            grouped[n] = stream.tile([P, WIDTH, PACK], BF16, name="grouped", align_bytes=64)
+            for copy, lo, hi in ((nc.scalar.copy, 0, scalar_cols), (nc.vector.tensor_copy, scalar_cols, WIDTH)):
+                source = raw[n][1 if lo == 0 else 0][:] if n == 0 else raw[n][:, :, lo:hi]
+                copy(
+                    out=grouped[n][:, lo:hi, :].rearrange("p (c i) t -> p c t i", i=RUN),
+                    in_=source.rearrange("p t (c i) -> p c t i", i=RUN),
+                )
+
+        def quantize(n):
+            codes[chunks[n]] = keep.tile([P, WIDTH], U32, name="codes%d" % n, align_bytes=64)
+            scales[chunks[n]] = keep.tile([P, WIDTH], U8, name="scales%d" % n, align_bytes=64)
+            nc.vector.quantize_mx(
+                out=codes[chunks[n]][:].bitcast(FP8X4),
+                scales=scales[chunks[n]][:],
+                in_=grouped[n][:].rearrange("p w t -> p (w t)"),
+            )
+
+        acc = {}
+
+        def multiply(i, half):
+            for ct in range(C_TILES):
+                if i == 0:
+                    acc[half, ct] = bank(half * C_TILES + ct, [P, WIDTH], F32)
+                cols = slice(ct * P, (ct + 1) * P)
+                nc.tensor.matmul_mx(
+                    out=acc[half, ct][:],
+                    lhsT=codes["assign", i, 0][:, cols].bitcast(FP8X4),
+                    lhsT_scale=scales["assign", i, 0][:, cols],
+                    rhs=codes["x", i, half][:].bitcast(FP8X4),
+                    rhs_scale=scales["x", i, half][:],
+                    start=(i == 0),
+                    stop=(i == PASSES - 1),
+                )
+
+        columns = keep.tile([P, VECTOR_ROWS], BF16, name="columns")
+        inv_size = keep.tile([P, C_TILES], F32, name="inv_size")
+        shift_all = keep.tile([P, FEATS], BF16, name="shift_all")
+        gain_all = keep.tile([P, FEATS], BF16, name="gain_all")
+
+        turned = bank(C_TILES, [P, P], BF16)
+        nc.tensor.transpose(turned[:], rows[:], ident_bf16[:])
+
+        def turn_vectors():
+            nc.vector.tensor_copy(out=columns[:], in_=turned[:, 0:VECTOR_ROWS])
+
+        def invert_sizes():
+            nc.vector.reciprocal(out=inv_size[:], in_=columns[:, SIZE_ROW:SHIFT_ROW])
+
+        def spread(index, first_row):
+            copies = bank(index, [P, FEATS], BF16)
+            for m in range(FEATS // P):
+                column = columns[:, first_row + m:first_row + m + 1]
+                nc.tensor.transpose(copies[:, m * P:(m + 1) * P], column.to_broadcast([P, P]), ident_bf16[:])
+            return copies
+
+        y = {}
+        y_pairs = {}
+        turned_pairs = {}
+        y_grouped = {}
+        y_codes = [keep.tile([P, CLUSTERS], U32, name="y_codes%d" % g, align_bytes=64) for g in range(HALVES)]
+        y_scales = [keep.tile([P, CLUSTERS], U8, name="y_scales%d" % g, align_bytes=64) for g in range(HALVES)]
+
+        def pool_and_shift(half, ct):
+            y[half, ct] = keep.tile([P, WIDTH], F32, name="y%d_%d" % (half, ct))
+            nc.vector.scalar_tensor_tensor(
+                out=y[half, ct][:],
+                in0=acc[half, ct][:],
+                scalar=inv_size[:, ct:ct + 1],
+                in1=shift_all[:, half * WIDTH:(half + 1) * WIDTH],
+                op0=ALU.mult,
+                op1=ALU.add,
+            )
+
+        def apply_gain(half, ct):
+            nc.vector.tensor_tensor(
+                out=y[half, ct][:],
+                in0=y[half, ct][:],
+                in1=gain_all[:, half * WIDTH:(half + 1) * WIDTH],
+                op=ALU.mult,
+            )
+            nc.sync.dma_start(
+                out=out_0[ct * P:(ct + 1) * P, half * WIDTH:(half + 1) * WIDTH], in_=y[half, ct][:]
+            )
+
+        def by_pairs(ap):
+            return ap.rearrange("c (p u e) -> c u p e", u=2, e=2)
+
+        def round_y(half, ct):
+            y_pairs[half, ct] = stream.tile([P, 2, P, 2], BF16, name="y_pairs")
+            nc.scalar.copy(out=y_pairs[half, ct][:], in_=by_pairs(y[half, ct][:]))
+
+        def apply_gain_rounded(half, ct):
+            y_pairs[half, ct] = stream.tile([P, 2, P, 2], BF16, name="y_pairs")
+            nc.vector.tensor_tensor(
+                out=y_pairs[half, ct][:],
+                in0=by_pairs(y[half, ct][:]),
+                in1=by_pairs(gain_all[:, half * WIDTH:(half + 1) * WIDTH]),
+                op=ALU.mult,
+            )
+
+        def turn_pairs(half, ct):
+            words = y_pairs[half, ct][:].rearrange("c u p e -> c (u p e)").bitcast(F32)
+            turned_pairs[half, ct] = bank(ct, [P, 2, P], F32)
+            for u in range(2):
+                nc.tensor.transpose(turned_pairs[half, ct][:, u, :], words[:, u * P:(u + 1) * P], ident_f32[:])
+
+        def join_pairs(half, ct):
+            y_grouped[half, ct] = stream.tile([P, P * PACK], BF16, name="y_grouped", align_bytes=64)
+            nc.scalar.copy(
+                out=y_grouped[half, ct][:].bitcast(F32).rearrange("p (c u) -> p c u", u=2),
+                in_=turned_pairs[half, ct][:].rearrange("p u c -> p c u"),
+            )
+
+        def quantize_y(half, ct):
+            cols = slice(ct * P, (ct + 1) * P)
+            nc.vector.quantize_mx(
+                out=y_codes[half][:, cols].bitcast(FP8X4),
+                scales=y_scales[half][:, cols],
+                in_=y_grouped[half, ct][:],
+            )
+
+        def store_planes(half):
+            nc.sync.dma_start(
+                out=out_1[half].rearrange("p m t -> p (m t)").bitcast(I32), in_=y_codes[half][:].bitcast(I32)
+            )
+            for q in range(4):
+                queue = nc.scalar if half == HALVES - 1 and q % 2 == 0 else nc.sync
+                queue.dma_start(
+                    out=out_2[half, 4 * q:4 * q + 4, :].bitcast(I32),
+                    in_=y_scales[half][32 * q:32 * q + 4, :].bitcast(I32),
+                )
+
+        first_epilogue = 2 * PASSES + 1
+        for n in range(len(chunks) + 1):
+            ct = n - first_epilogue
+            if n < len(chunks):
+                interleave(n, SCALAR_COLS_EPILOGUE if 0 <= ct < C_TILES else SCALAR_COLS)
+            if 0 <= ct < C_TILES:
+                pool_and_shift(0, ct)
+            if 0 <= ct - 2 < C_TILES:
+                join_pairs(0, ct - 2)
+            if n >= 1:
+                quantize(n - 1)
+                kind, i, half = chunks[n - 1]
+                if kind == "assign" or half == 1:
+                    multiply(i, half)
+            if 0 <= ct < C_TILES:
+                apply_gain(0, ct)
+            if 0 <= ct - 1 < C_TILES:
+                round_y(0, ct - 1)
+                turn_pairs(0, ct - 1)
+            if 0 <= ct - 4 < C_TILES:
+                quantize_y(0, ct - 4)
+            if n == 1:
+                turn_vectors()
+                shift_copies = spread(C_TILES + 1, SHIFT_ROW)
+                gain_copies = spread(C_TILES + 2, GAIN_ROW)
+            if n == 2:
+                invert_sizes()
+            if n == 4:
+                nc.scalar.copy(out=shift_all[:], in_=shift_copies[:])
+            if n == 6:
+                nc.scalar.copy(out=gain_all[:], in_=gain_copies[:])
+        store_planes(0)
+
+        last = HALVES - 1
+        final = C_TILES - 1
+        for step in range(C_TILES):
+            pool_and_shift(last, step)
+            if step >= 1:
+                apply_gain(last, step - 1)
+                round_y(last, step - 1)
+                turn_pairs(last, step - 1)
+            if step >= 2:
+                join_pairs(last, step - 2)
+        quantize_y(last, 0)
+        apply_gain_rounded(last, final)
+        join_pairs(last, final - 1)
+        turn_pairs(last, final)
+        apply_gain(last, final)
+        join_pairs(last, final)
+        for ct in range(1, C_TILES):
+            quantize_y(last, ct)
+        store_planes(last)

@@ -22,8 +22,10 @@ WIDTH = 512
 HALVES = FEATS // WIDTH
 C_TILES = CLUSTERS // P
 RUN = 4
-SCALAR_COLS = 256
-SCALAR_COLS_EPILOGUE = 320
+SCALAR_COLS_START = 256
+SCALAR_COLS_FIRST_HALF = 512
+SCALAR_COLS_SECOND_HALF = 328
+SCALAR_COLS_END = 312
 SIZE_ROW = 0
 SHIFT_ROW = SIZE_ROW + C_TILES
 GAIN_ROW = SHIFT_ROW + FEATS // P
@@ -42,15 +44,19 @@ def tile_cluster_mean_pool_g1_kernel(tc, assign, x, sizes, shift, gain, out_0, o
         def bank(index, shape, dtype):
             return psum.tile(shape, dtype, name="bank%d" % index, tag="bank%d" % index)
 
-        chunks = []
+        steps = []
         for i in range(PASSES):
-            chunks.append(("x", i, 0))
-            chunks.append(("assign", i, 0))
+            if i < 0:
+                steps.append(([("x", i, 0)], SCALAR_COLS_START))
+                steps.append(([("assign", i, 0)], SCALAR_COLS_START))
+            else:
+                steps.append(([("assign", i, 0), ("x", i, 0)], SCALAR_COLS_FIRST_HALF))
+        first_half_steps = len(steps)
         for i in range(PASSES):
-            chunks.append(("x", i, 1))
+            steps.append(([("x", i, 1)], SCALAR_COLS_SECOND_HALF if i < PASSES - 1 else SCALAR_COLS_END))
 
         rows = keep.tile([P, P], BF16, name="rows")
-        nc.vector.memset(rows[:], 0.0)
+        nc.gpsimd.memset(rows[:], 0.0)
         nc.scalar.dma_start(out=rows[SIZE_ROW:SHIFT_ROW, :], in_=sizes.rearrange("(j p) -> j p", p=P))
         nc.scalar.dma_start(out=rows[SHIFT_ROW:GAIN_ROW, :], in_=shift.rearrange("(j p) -> j p", p=P))
         nc.scalar.dma_start(out=rows[GAIN_ROW:VECTOR_ROWS, :], in_=gain.rearrange("(j p) -> j p", p=P))
@@ -59,44 +65,50 @@ def tile_cluster_mean_pool_g1_kernel(tc, assign, x, sizes, shift, gain, out_0, o
         make_identity(nc, ident_bf16[:])
         make_identity(nc, ident_f32[:])
 
-        raw = []
-        for n, (kind, i, half) in enumerate(chunks):
+        raw = {}
+
+        def load(chunk, lo, hi):
+            kind, i, half = chunk
             source = assign if kind == "assign" else x
-            block = source[i * K_PASS:(i + 1) * K_PASS, half * WIDTH:(half + 1) * WIDTH]
-            block = block.rearrange("(p j) w -> p j w", j=PACK)
-            if n == 0:
-                parts = []
-                for lo, hi in ((SCALAR_COLS, WIDTH), (0, SCALAR_COLS)):
-                    loaded = keep.tile([P, PACK, hi - lo], BF16, name="raw0_%d" % lo)
-                    nc.sync.dma_start(out=loaded[:], in_=block[:, :, lo:hi])
-                    parts.append(loaded)
-                raw.append(parts)
-            else:
-                loaded = keep.tile([P, PACK, WIDTH], BF16, name="raw%d" % n)
-                nc.sync.dma_start(out=loaded[:], in_=block)
-                raw.append(loaded)
+            block = source[i * K_PASS:(i + 1) * K_PASS, half * WIDTH + lo:half * WIDTH + hi]
+            loaded = keep.tile([P, PACK, hi - lo], BF16, name="raw_%s%d_%d_%d" % (kind, i, half, lo))
+            nc.sync.dma_start(out=loaded[:], in_=block.rearrange("(p j) w -> p j w", j=PACK))
+            raw.setdefault(chunk, []).append((lo, hi, loaded))
+
+        for n, (chunks, scalar_cols) in enumerate(steps):
+            for chunk in chunks[::-1]:
+                load(chunk, 0, WIDTH)
 
         grouped = {}
         codes = {}
         scales = {}
 
-        def interleave(n, scalar_cols):
-            grouped[n] = stream.tile([P, WIDTH, PACK], BF16, name="grouped", align_bytes=64)
-            for copy, lo, hi in ((nc.scalar.copy, 0, scalar_cols), (nc.vector.tensor_copy, scalar_cols, WIDTH)):
-                source = raw[n][1 if lo == 0 else 0][:] if n == 0 else raw[n][:, :, lo:hi]
-                copy(
-                    out=grouped[n][:, lo:hi, :].rearrange("p (c i) t -> p c t i", i=RUN),
-                    in_=source.rearrange("p t (c i) -> p c t i", i=RUN),
-                )
+        def interleave(n):
+            chunks, scalar_cols = steps[n]
+            grouped[n] = stream.tile([P, len(chunks) * WIDTH, PACK], BF16, name="grouped", align_bytes=64, bufs=4)
+            for place, chunk in enumerate(chunks):
+                cut = min(max(scalar_cols - place * WIDTH, 0), WIDTH)
+                for copy, lo, hi in ((nc.scalar.copy, 0, cut), (nc.vector.tensor_copy, cut, WIDTH)):
+                    for first, end, loaded in raw[chunk]:
+                        if lo < hi and first <= lo and hi <= end:
+                            target = grouped[n][:, place * WIDTH + lo:place * WIDTH + hi, :]
+                            copy(
+                                out=target.rearrange("p (c i) t -> p c t i", i=RUN),
+                                in_=loaded[:, :, lo - first:hi - first].rearrange("p t (c i) -> p c t i", i=RUN),
+                            )
 
         def quantize(n):
-            codes[chunks[n]] = keep.tile([P, WIDTH], U32, name="codes%d" % n, align_bytes=64)
-            scales[chunks[n]] = keep.tile([P, WIDTH], U8, name="scales%d" % n, align_bytes=64)
+            chunks = steps[n][0]
+            step_codes = keep.tile([P, len(chunks) * WIDTH], U32, name="codes%d" % n, align_bytes=64)
+            step_scales = keep.tile([P, len(chunks) * WIDTH], U8, name="scales%d" % n, align_bytes=64)
             nc.vector.quantize_mx(
-                out=codes[chunks[n]][:].bitcast(FP8X4),
-                scales=scales[chunks[n]][:],
+                out=step_codes[:].bitcast(FP8X4),
+                scales=step_scales[:],
                 in_=grouped[n][:].rearrange("p w t -> p (w t)"),
             )
+            for place, chunk in enumerate(chunks):
+                codes[chunk] = step_codes[:, place * WIDTH:(place + 1) * WIDTH]
+                scales[chunk] = step_scales[:, place * WIDTH:(place + 1) * WIDTH]
 
         acc = {}
 
@@ -109,25 +121,22 @@ def tile_cluster_mean_pool_g1_kernel(tc, assign, x, sizes, shift, gain, out_0, o
                     out=acc[half, ct][:],
                     lhsT=codes["assign", i, 0][:, cols].bitcast(FP8X4),
                     lhsT_scale=scales["assign", i, 0][:, cols],
-                    rhs=codes["x", i, half][:].bitcast(FP8X4),
-                    rhs_scale=scales["x", i, half][:],
+                    rhs=codes["x", i, half].bitcast(FP8X4),
+                    rhs_scale=scales["x", i, half],
                     start=(i == 0),
                     stop=(i == PASSES - 1),
                 )
+
+        def quantize_and_multiply(n):
+            quantize(n)
+            for kind, i, half in steps[n][0]:
+                if kind == "assign" or half == 1:
+                    multiply(i, half)
 
         columns = keep.tile([P, VECTOR_ROWS], BF16, name="columns")
         inv_size = keep.tile([P, C_TILES], F32, name="inv_size")
         shift_all = keep.tile([P, FEATS], BF16, name="shift_all")
         gain_all = keep.tile([P, FEATS], BF16, name="gain_all")
-
-        turned = bank(C_TILES, [P, P], BF16)
-        nc.tensor.transpose(turned[:], rows[:], ident_bf16[:])
-
-        def turn_vectors():
-            nc.vector.tensor_copy(out=columns[:], in_=turned[:, 0:VECTOR_ROWS])
-
-        def invert_sizes():
-            nc.vector.reciprocal(out=inv_size[:], in_=columns[:, SIZE_ROW:SHIFT_ROW])
 
         def spread(index, first_row):
             copies = bank(index, [P, FEATS], BF16)
@@ -139,9 +148,9 @@ def tile_cluster_mean_pool_g1_kernel(tc, assign, x, sizes, shift, gain, out_0, o
         y = {}
         y_pairs = {}
         turned_pairs = {}
-        y_grouped = {}
+        y_grouped = [keep.tile([P, CLUSTERS * PACK], BF16, name="y_grouped%d" % g, align_bytes=64) for g in range(HALVES)]
         y_codes = [keep.tile([P, CLUSTERS], U32, name="y_codes%d" % g, align_bytes=64) for g in range(HALVES)]
-        y_scales = [keep.tile([P, CLUSTERS], U8, name="y_scales%d" % g, align_bytes=64) for g in range(HALVES)]
+        y_scales = keep.tile([P, CLUSTERS], U8, name="y_scales", align_bytes=64)
 
         def pool_and_shift(half, ct):
             y[half, ct] = keep.tile([P, WIDTH], F32, name="y%d_%d" % (half, ct))
@@ -154,13 +163,15 @@ def tile_cluster_mean_pool_g1_kernel(tc, assign, x, sizes, shift, gain, out_0, o
                 op1=ALU.add,
             )
 
-        def apply_gain(half, ct):
-            nc.vector.tensor_tensor(
-                out=y[half, ct][:],
-                in0=y[half, ct][:],
-                in1=gain_all[:, half * WIDTH:(half + 1) * WIDTH],
+        def apply_gain(engine, half, ct, lo, hi):
+            engine.tensor_tensor(
+                out=y[half, ct][:, lo:hi],
+                in0=y[half, ct][:, lo:hi],
+                in1=gain_all[:, half * WIDTH + lo:half * WIDTH + hi],
                 op=ALU.mult,
             )
+
+        def store_y(half, ct):
             nc.sync.dma_start(
                 out=out_0[ct * P:(ct + 1) * P, half * WIDTH:(half + 1) * WIDTH], in_=y[half, ct][:]
             )
@@ -182,86 +193,97 @@ def tile_cluster_mean_pool_g1_kernel(tc, assign, x, sizes, shift, gain, out_0, o
             )
 
         def turn_pairs(half, ct):
-            words = y_pairs[half, ct][:].rearrange("c u p e -> c (u p e)").bitcast(F32)
             turned_pairs[half, ct] = bank(ct, [P, 2, P], F32)
+            words = y_pairs[half, ct][:].rearrange("c u p e -> c (u p e)").bitcast(F32)
             for u in range(2):
                 nc.tensor.transpose(turned_pairs[half, ct][:, u, :], words[:, u * P:(u + 1) * P], ident_f32[:])
 
-        def join_pairs(half, ct):
-            y_grouped[half, ct] = stream.tile([P, P * PACK], BF16, name="y_grouped", align_bytes=64)
-            nc.scalar.copy(
-                out=y_grouped[half, ct][:].bitcast(F32).rearrange("p (c u) -> p c u", u=2),
+        def join_pairs(copy, half, ct):
+            target = y_grouped[half][:, ct * P * PACK:(ct + 1) * P * PACK]
+            copy(
+                out=target.bitcast(F32).rearrange("p (c u) -> p c u", u=2),
                 in_=turned_pairs[half, ct][:].rearrange("p u c -> p c u"),
             )
 
-        def quantize_y(half, ct):
-            cols = slice(ct * P, (ct + 1) * P)
+        def quantize_y(half, first, count):
+            cols = slice(first * P, (first + count) * P)
             nc.vector.quantize_mx(
                 out=y_codes[half][:, cols].bitcast(FP8X4),
-                scales=y_scales[half][:, cols],
-                in_=y_grouped[half, ct][:],
+                scales=y_scales[4 * half:P, cols],
+                in_=y_grouped[half][:, first * P * PACK:(first + count) * P * PACK],
             )
 
-        def store_planes(half):
+        def store_codes(half, lo, hi):
             nc.sync.dma_start(
-                out=out_1[half].rearrange("p m t -> p (m t)").bitcast(I32), in_=y_codes[half][:].bitcast(I32)
+                out=out_1[half, :, lo:hi, :].rearrange("p m t -> p (m t)").bitcast(I32),
+                in_=y_codes[half][:, lo:hi].bitcast(I32),
             )
+
+        def store_scales():
             for q in range(4):
-                queue = nc.scalar if half == HALVES - 1 and q % 2 == 0 else nc.sync
+                queue = nc.scalar if q % 2 == 0 else nc.sync
                 queue.dma_start(
-                    out=out_2[half, 4 * q:4 * q + 4, :].bitcast(I32),
-                    in_=y_scales[half][32 * q:32 * q + 4, :].bitcast(I32),
+                    out=out_2[:, 4 * q:4 * q + 4, :].bitcast(I32),
+                    in_=y_scales[32 * q:32 * q + 4 * HALVES, :].bitcast(I32),
                 )
 
-        first_epilogue = 2 * PASSES + 1
-        for n in range(len(chunks) + 1):
-            ct = n - first_epilogue
-            if n < len(chunks):
-                interleave(n, SCALAR_COLS_EPILOGUE if 0 <= ct < C_TILES else SCALAR_COLS)
-            if 0 <= ct < C_TILES:
-                pool_and_shift(0, ct)
-            if 0 <= ct - 2 < C_TILES:
-                join_pairs(0, ct - 2)
-            if n >= 1:
-                quantize(n - 1)
-                kind, i, half = chunks[n - 1]
-                if kind == "assign" or half == 1:
-                    multiply(i, half)
-            if 0 <= ct < C_TILES:
-                apply_gain(0, ct)
-            if 0 <= ct - 1 < C_TILES:
-                round_y(0, ct - 1)
-                turn_pairs(0, ct - 1)
-            if 0 <= ct - 4 < C_TILES:
-                quantize_y(0, ct - 4)
-            if n == 1:
-                turn_vectors()
-                shift_copies = spread(C_TILES + 1, SHIFT_ROW)
-                gain_copies = spread(C_TILES + 2, GAIN_ROW)
-            if n == 2:
-                invert_sizes()
-            if n == 4:
-                nc.scalar.copy(out=shift_all[:], in_=shift_copies[:])
-            if n == 6:
-                nc.scalar.copy(out=gain_all[:], in_=gain_copies[:])
-        store_planes(0)
+        turned = bank(C_TILES, [P, P], BF16)
+        nc.tensor.transpose(turned[:], rows[:], ident_bf16[:])
 
+        nc.vector.tensor_copy(out=columns[:], in_=turned[:, 0:VECTOR_ROWS])
+        shift_copies = spread(C_TILES + 1, SHIFT_ROW)
+        gain_copies = spread(C_TILES + 2, GAIN_ROW)
+        for n in range(len(steps)):
+            interleave(n)
+            late = n - first_half_steps
+            if late in (4, 6):
+                round_y(0, late // 2 - 2)
+            if n >= 1:
+                quantize_and_multiply(n - 1)
+            if late in (5, 7):
+                turn_pairs(0, late // 2 - 2)
+            if late >= 1 and late % 2 == 1:
+                pool_and_shift(0, late // 2)
+            if late >= 2 and late % 2 == 0:
+                apply_gain(nc.vector, 0, late // 2 - 1, 0, WIDTH)
+                store_y(0, late // 2 - 1)
+            if n == 0:
+                nc.vector.reciprocal(out=inv_size[:], in_=columns[:, SIZE_ROW:SHIFT_ROW])
+            if n == 0:
+                nc.vector.tensor_copy(out=shift_all[:], in_=shift_copies[:])
+            if n == 0:
+                nc.vector.tensor_copy(out=gain_all[:], in_=gain_copies[:])
         last = HALVES - 1
         final = C_TILES - 1
-        for step in range(C_TILES):
-            pool_and_shift(last, step)
-            if step >= 1:
-                apply_gain(last, step - 1)
-                round_y(last, step - 1)
-                turn_pairs(last, step - 1)
-            if step >= 2:
-                join_pairs(last, step - 2)
-        quantize_y(last, 0)
-        apply_gain_rounded(last, final)
-        join_pairs(last, final - 1)
-        turn_pairs(last, final)
-        apply_gain(last, final)
-        join_pairs(last, final)
+        quantize_and_multiply(len(steps) - 1)
+        apply_gain(nc.vector, 0, final, 0, WIDTH)
+        store_y(0, final)
+        round_y(0, final - 1)
+        turn_pairs(0, final - 1)
+        join_pairs(nc.scalar.copy, 0, 0)
+        round_y(0, final)
+        turn_pairs(0, final)
         for ct in range(1, C_TILES):
-            quantize_y(last, ct)
-        store_planes(last)
+            join_pairs(nc.scalar.copy, 0, ct)
+        for ct in range(C_TILES):
+            pool_and_shift(last, ct)
+            if ct >= 1:
+                apply_gain(nc.vector, last, ct - 1, 0, WIDTH)
+                store_y(last, ct - 1)
+                round_y(last, ct - 1)
+                turn_pairs(last, ct - 1)
+            if ct >= 2:
+                join_pairs(nc.scalar.copy, last, ct - 2)
+        apply_gain_rounded(last, final)
+        join_pairs(nc.scalar.copy, last, final - 1)
+        turn_pairs(last, final)
+        apply_gain(nc.vector, last, final, 0, WIDTH)
+        store_y(last, final)
+        join_pairs(nc.scalar.copy, last, final)
+        quantize_y(0, 0, C_TILES)
+        store_codes(0, 0, CLUSTERS)
+        quantize_y(last, 0, 2)
+        store_codes(last, 0, 2 * P)
+        quantize_y(last, 2, 2)
+        store_codes(last, 2 * P, CLUSTERS)
+        store_scales()

@@ -21,15 +21,19 @@ PASSES = NODES // K_PASS
 WIDTH = 512
 HALVES = FEATS // WIDTH
 C_TILES = CLUSTERS // P
+QUADRANT = 32
+SCALE_ROWS = 4
+
 RUN = 4
-SCALAR_COLS_START = 256
-SCALAR_COLS_FIRST_HALF = 512
-SCALAR_COLS_SECOND_HALF = 328
-SCALAR_COLS_END = 312
-SIZE_ROW = 0
-SHIFT_ROW = SIZE_ROW + C_TILES
+WHOLE_PASSES = 4
+assert PASSES - WHOLE_PASSES == C_TILES
+SCALAR_COLS_EARLY = 256
+SCALAR_COLS_LATE = 456
+SCALAR_COLS_END = 424
+
+SIZE_ROW = QUADRANT - (CLUSTERS + 2 * FEATS) // P
+SHIFT_ROW = SIZE_ROW + CLUSTERS // P
 GAIN_ROW = SHIFT_ROW + FEATS // P
-VECTOR_ROWS = GAIN_ROW + FEATS // P
 
 
 def tile_cluster_mean_pool_g1_kernel(tc, assign, x, sizes, shift, gain, out_0, out_1, out_2):
@@ -44,96 +48,85 @@ def tile_cluster_mean_pool_g1_kernel(tc, assign, x, sizes, shift, gain, out_0, o
         def bank(index, shape, dtype):
             return psum.tile(shape, dtype, name="bank%d" % index, tag="bank%d" % index)
 
-        steps = []
+        chunks = []
         for i in range(PASSES):
-            if i < 0:
-                steps.append(([("x", i, 0)], SCALAR_COLS_START))
-                steps.append(([("assign", i, 0)], SCALAR_COLS_START))
-            else:
-                steps.append(([("assign", i, 0), ("x", i, 0)], SCALAR_COLS_FIRST_HALF))
-        first_half_steps = len(steps)
-        for i in range(PASSES):
-            steps.append(([("x", i, 1)], SCALAR_COLS_SECOND_HALF if i < PASSES - 1 else SCALAR_COLS_END))
+            chunks.append(("assign", i, 0))
+            chunks.append(("x", i, 0))
+            if i < WHOLE_PASSES:
+                chunks.append(("x", i, 1))
+        early_chunks = len(chunks)
+        for i in range(WHOLE_PASSES, PASSES):
+            chunks.append(("x", i, 1))
+
+        def scalar_cols(n):
+            if n <= early_chunks:
+                return SCALAR_COLS_EARLY
+            if n < len(chunks) - 1:
+                return SCALAR_COLS_LATE
+            return SCALAR_COLS_END
 
         rows = keep.tile([P, P], BF16, name="rows")
-        nc.gpsimd.memset(rows[:], 0.0)
-        nc.scalar.dma_start(out=rows[SIZE_ROW:SHIFT_ROW, :], in_=sizes.rearrange("(j p) -> j p", p=P))
-        nc.scalar.dma_start(out=rows[SHIFT_ROW:GAIN_ROW, :], in_=shift.rearrange("(j p) -> j p", p=P))
-        nc.scalar.dma_start(out=rows[GAIN_ROW:VECTOR_ROWS, :], in_=gain.rearrange("(j p) -> j p", p=P))
+        nc.sync.dma_start(out=rows[SIZE_ROW:SHIFT_ROW, :], in_=sizes.rearrange("(j p) -> j p", p=P))
+        nc.sync.dma_start(out=rows[SHIFT_ROW:GAIN_ROW, :], in_=shift.rearrange("(j p) -> j p", p=P))
+        nc.sync.dma_start(out=rows[GAIN_ROW:QUADRANT, :], in_=gain.rearrange("(j p) -> j p", p=P))
+        for lo, hi in ((0, SIZE_ROW), (QUADRANT, 2 * QUADRANT), (2 * QUADRANT, P)):
+            nc.gpsimd.memset(rows[lo:hi, :], 0.0)
         ident_bf16 = keep.tile([P, P], BF16, name="ident_bf16")
         ident_f32 = keep.tile([P, P], F32, name="ident_f32")
         make_identity(nc, ident_bf16[:])
         make_identity(nc, ident_f32[:])
 
         raw = {}
-
-        def load(chunk, lo, hi):
+        for chunk in chunks:
             kind, i, half = chunk
-            source = assign if kind == "assign" else x
-            block = source[i * K_PASS:(i + 1) * K_PASS, half * WIDTH + lo:half * WIDTH + hi]
-            loaded = keep.tile([P, PACK, hi - lo], BF16, name="raw_%s%d_%d_%d" % (kind, i, half, lo))
-            nc.sync.dma_start(out=loaded[:], in_=block.rearrange("(p j) w -> p j w", j=PACK))
-            raw.setdefault(chunk, []).append((lo, hi, loaded))
-
-        for n, (chunks, scalar_cols) in enumerate(steps):
-            for chunk in chunks[::-1]:
-                load(chunk, 0, WIDTH)
+            if chunk not in raw:
+                source = assign if kind == "assign" else x
+                count = HALVES if kind == "x" and i < WHOLE_PASSES else 1
+                block = source[i * K_PASS:(i + 1) * K_PASS, half * WIDTH:(half + count) * WIDTH]
+                loaded = keep.tile([P, PACK, count * WIDTH], BF16, name="raw_%s%d_%d" % chunk)
+                nc.sync.dma_start(out=loaded[:], in_=block.rearrange("(p t) w -> p t w", t=PACK))
+                for k in range(count):
+                    raw[kind, i, half + k] = loaded[:, :, k * WIDTH:(k + 1) * WIDTH]
 
         grouped = {}
         codes = {}
         scales = {}
-
-        def interleave(n):
-            chunks, scalar_cols = steps[n]
-            grouped[n] = stream.tile([P, len(chunks) * WIDTH, PACK], BF16, name="grouped", align_bytes=64, bufs=4)
-            for place, chunk in enumerate(chunks):
-                cut = min(max(scalar_cols - place * WIDTH, 0), WIDTH)
-                for copy, lo, hi in ((nc.scalar.copy, 0, cut), (nc.vector.tensor_copy, cut, WIDTH)):
-                    for first, end, loaded in raw[chunk]:
-                        if lo < hi and first <= lo and hi <= end:
-                            target = grouped[n][:, place * WIDTH + lo:place * WIDTH + hi, :]
-                            copy(
-                                out=target.rearrange("p (c i) t -> p c t i", i=RUN),
-                                in_=loaded[:, :, lo - first:hi - first].rearrange("p t (c i) -> p c t i", i=RUN),
-                            )
-
-        def quantize(n):
-            chunks = steps[n][0]
-            step_codes = keep.tile([P, len(chunks) * WIDTH], U32, name="codes%d" % n, align_bytes=64)
-            step_scales = keep.tile([P, len(chunks) * WIDTH], U8, name="scales%d" % n, align_bytes=64)
-            nc.vector.quantize_mx(
-                out=step_codes[:].bitcast(FP8X4),
-                scales=step_scales[:],
-                in_=grouped[n][:].rearrange("p w t -> p (w t)"),
-            )
-            for place, chunk in enumerate(chunks):
-                codes[chunk] = step_codes[:, place * WIDTH:(place + 1) * WIDTH]
-                scales[chunk] = step_scales[:, place * WIDTH:(place + 1) * WIDTH]
-
         acc = {}
 
-        def multiply(i, half):
-            for ct in range(C_TILES):
-                if i == 0:
-                    acc[half, ct] = bank(half * C_TILES + ct, [P, WIDTH], F32)
-                cols = slice(ct * P, (ct + 1) * P)
-                nc.tensor.matmul_mx(
-                    out=acc[half, ct][:],
-                    lhsT=codes["assign", i, 0][:, cols].bitcast(FP8X4),
-                    lhsT_scale=scales["assign", i, 0][:, cols],
-                    rhs=codes["x", i, half].bitcast(FP8X4),
-                    rhs_scale=scales["x", i, half],
-                    start=(i == 0),
-                    stop=(i == PASSES - 1),
+        def interleave(n):
+            cut = scalar_cols(n)
+            grouped[n] = stream.tile([P, WIDTH, PACK], BF16, name="grouped", align_bytes=64)
+            for copy, lo, hi in ((nc.scalar.copy, 0, cut), (nc.vector.tensor_copy, cut, WIDTH)):
+                copy(
+                    out=grouped[n][:, lo:hi, :].rearrange("p (c i) t -> p c t i", i=RUN),
+                    in_=raw[chunks[n]][:, :, lo:hi].rearrange("p t (c i) -> p c t i", i=RUN),
                 )
 
         def quantize_and_multiply(n):
-            quantize(n)
-            for kind, i, half in steps[n][0]:
-                if kind == "assign" or half == 1:
-                    multiply(i, half)
+            kind, i, half = chunks[n]
+            codes[chunks[n]] = keep.tile([P, WIDTH], U32, name="codes%d" % n, align_bytes=64)
+            scales[chunks[n]] = keep.tile([P, WIDTH], U8, name="scales%d" % n, align_bytes=64)
+            nc.vector.quantize_mx(
+                out=codes[chunks[n]][:].bitcast(FP8X4),
+                scales=scales[chunks[n]][:],
+                in_=grouped[n][:].rearrange("p w t -> p (w t)"),
+            )
+            if kind == "x":
+                for ct in range(C_TILES):
+                    if i == 0:
+                        acc[half, ct] = bank(half * C_TILES + ct, [P, WIDTH], F32)
+                    cols = slice(ct * P, (ct + 1) * P)
+                    nc.tensor.matmul_mx(
+                        out=acc[half, ct][:],
+                        lhsT=codes["assign", i, 0][:, cols].bitcast(FP8X4),
+                        lhsT_scale=scales["assign", i, 0][:, cols],
+                        rhs=codes["x", i, half][:].bitcast(FP8X4),
+                        rhs_scale=scales["x", i, half][:],
+                        start=(i == 0),
+                        stop=(i == PASSES - 1),
+                    )
 
-        columns = keep.tile([P, VECTOR_ROWS], BF16, name="columns")
+        columns = keep.tile([P, QUADRANT], BF16, name="columns")
         inv_size = keep.tile([P, C_TILES], F32, name="inv_size")
         shift_all = keep.tile([P, FEATS], BF16, name="shift_all")
         gain_all = keep.tile([P, FEATS], BF16, name="gain_all")
@@ -148,8 +141,10 @@ def tile_cluster_mean_pool_g1_kernel(tc, assign, x, sizes, shift, gain, out_0, o
         y = {}
         y_pairs = {}
         turned_pairs = {}
-        y_grouped = [keep.tile([P, CLUSTERS * PACK], BF16, name="y_grouped%d" % g, align_bytes=64) for g in range(HALVES)]
-        y_codes = [keep.tile([P, CLUSTERS], U32, name="y_codes%d" % g, align_bytes=64) for g in range(HALVES)]
+        y_grouped = [
+            keep.tile([P, CLUSTERS * PACK], BF16, name="y_grouped%d" % half, align_bytes=64) for half in range(HALVES)
+        ]
+        y_codes = [keep.tile([P, CLUSTERS], U32, name="y_codes%d" % half, align_bytes=64) for half in range(HALVES)]
         y_scales = keep.tile([P, CLUSTERS], U8, name="y_scales", align_bytes=64)
 
         def pool_and_shift(half, ct):
@@ -163,18 +158,14 @@ def tile_cluster_mean_pool_g1_kernel(tc, assign, x, sizes, shift, gain, out_0, o
                 op1=ALU.add,
             )
 
-        def apply_gain(engine, half, ct, lo, hi):
-            engine.tensor_tensor(
-                out=y[half, ct][:, lo:hi],
-                in0=y[half, ct][:, lo:hi],
-                in1=gain_all[:, half * WIDTH + lo:half * WIDTH + hi],
+        def apply_gain(half, ct):
+            nc.vector.tensor_tensor(
+                out=y[half, ct][:],
+                in0=y[half, ct][:],
+                in1=gain_all[:, half * WIDTH:(half + 1) * WIDTH],
                 op=ALU.mult,
             )
-
-        def store_y(half, ct):
-            nc.sync.dma_start(
-                out=out_0[ct * P:(ct + 1) * P, half * WIDTH:(half + 1) * WIDTH], in_=y[half, ct][:]
-            )
+            nc.sync.dma_start(out=out_0[ct * P:(ct + 1) * P, half * WIDTH:(half + 1) * WIDTH], in_=y[half, ct][:])
 
         def by_pairs(ap):
             return ap.rearrange("c (p u e) -> c u p e", u=2, e=2)
@@ -194,13 +185,13 @@ def tile_cluster_mean_pool_g1_kernel(tc, assign, x, sizes, shift, gain, out_0, o
 
         def turn_pairs(half, ct):
             turned_pairs[half, ct] = bank(ct, [P, 2, P], F32)
-            words = y_pairs[half, ct][:].rearrange("c u p e -> c (u p e)").bitcast(F32)
+            pairs = y_pairs[half, ct][:].rearrange("c u p e -> c (u p e)").bitcast(F32)
             for u in range(2):
-                nc.tensor.transpose(turned_pairs[half, ct][:, u, :], words[:, u * P:(u + 1) * P], ident_f32[:])
+                nc.tensor.transpose(turned_pairs[half, ct][:, u, :], pairs[:, u * P:(u + 1) * P], ident_f32[:])
 
-        def join_pairs(copy, half, ct):
+        def join_pairs(half, ct):
             target = y_grouped[half][:, ct * P * PACK:(ct + 1) * P * PACK]
-            copy(
+            nc.scalar.copy(
                 out=target.bitcast(F32).rearrange("p (c u) -> p c u", u=2),
                 in_=turned_pairs[half, ct][:].rearrange("p u c -> p c u"),
             )
@@ -209,81 +200,67 @@ def tile_cluster_mean_pool_g1_kernel(tc, assign, x, sizes, shift, gain, out_0, o
             cols = slice(first * P, (first + count) * P)
             nc.vector.quantize_mx(
                 out=y_codes[half][:, cols].bitcast(FP8X4),
-                scales=y_scales[4 * half:P, cols],
+                scales=y_scales[SCALE_ROWS * half:P, cols],
                 in_=y_grouped[half][:, first * P * PACK:(first + count) * P * PACK],
             )
-
-        def store_codes(half, lo, hi):
             nc.sync.dma_start(
-                out=out_1[half, :, lo:hi, :].rearrange("p m t -> p (m t)").bitcast(I32),
-                in_=y_codes[half][:, lo:hi].bitcast(I32),
+                out=out_1[half, :, cols, :].rearrange("p m t -> p (m t)").bitcast(I32),
+                in_=y_codes[half][:, cols].bitcast(I32),
             )
 
-        def store_scales():
-            for q in range(4):
-                queue = nc.scalar if q % 2 == 0 else nc.sync
-                queue.dma_start(
-                    out=out_2[:, 4 * q:4 * q + 4, :].bitcast(I32),
-                    in_=y_scales[32 * q:32 * q + 4 * HALVES, :].bitcast(I32),
-                )
-
-        turned = bank(C_TILES, [P, P], BF16)
-        nc.tensor.transpose(turned[:], rows[:], ident_bf16[:])
-
-        nc.vector.tensor_copy(out=columns[:], in_=turned[:, 0:VECTOR_ROWS])
+        turned_rows = bank(C_TILES, [P, P], BF16)
+        nc.tensor.transpose(turned_rows[:], rows[:], ident_bf16[:])
+        nc.vector.tensor_copy(out=columns[:], in_=turned_rows[:, 0:QUADRANT])
         shift_copies = spread(C_TILES + 1, SHIFT_ROW)
         gain_copies = spread(C_TILES + 2, GAIN_ROW)
-        for n in range(len(steps)):
+
+        final = C_TILES - 1
+        for n in range(len(chunks)):
             interleave(n)
-            late = n - first_half_steps
-            if late in (4, 6):
-                round_y(0, late // 2 - 2)
+            late = n - early_chunks
+            if late == final:
+                round_y(0, 0)
             if n >= 1:
                 quantize_and_multiply(n - 1)
-            if late in (5, 7):
-                turn_pairs(0, late // 2 - 2)
-            if late >= 1 and late % 2 == 1:
-                pool_and_shift(0, late // 2)
-            if late >= 2 and late % 2 == 0:
-                apply_gain(nc.vector, 0, late // 2 - 1, 0, WIDTH)
-                store_y(0, late // 2 - 1)
+            if late == 1:
+                pool_and_shift(0, 0)
+            if late >= 1:
+                pool_and_shift(0, late)
+                apply_gain(0, late - 1)
             if n == 0:
                 nc.vector.reciprocal(out=inv_size[:], in_=columns[:, SIZE_ROW:SHIFT_ROW])
-            if n == 0:
                 nc.vector.tensor_copy(out=shift_all[:], in_=shift_copies[:])
-            if n == 0:
                 nc.vector.tensor_copy(out=gain_all[:], in_=gain_copies[:])
-        last = HALVES - 1
-        final = C_TILES - 1
-        quantize_and_multiply(len(steps) - 1)
-        apply_gain(nc.vector, 0, final, 0, WIDTH)
-        store_y(0, final)
-        round_y(0, final - 1)
-        turn_pairs(0, final - 1)
-        join_pairs(nc.scalar.copy, 0, 0)
-        round_y(0, final)
-        turn_pairs(0, final)
+        quantize_and_multiply(len(chunks) - 1)
+
+        apply_gain(0, final)
+        turn_pairs(0, 0)
         for ct in range(1, C_TILES):
-            join_pairs(nc.scalar.copy, 0, ct)
+            round_y(0, ct)
+            turn_pairs(0, ct)
         for ct in range(C_TILES):
-            pool_and_shift(last, ct)
+            join_pairs(0, ct)
+
+        for ct in range(C_TILES):
+            pool_and_shift(1, ct)
             if ct >= 1:
-                apply_gain(nc.vector, last, ct - 1, 0, WIDTH)
-                store_y(last, ct - 1)
-                round_y(last, ct - 1)
-                turn_pairs(last, ct - 1)
+                apply_gain(1, ct - 1)
+                round_y(1, ct - 1)
+                turn_pairs(1, ct - 1)
             if ct >= 2:
-                join_pairs(nc.scalar.copy, last, ct - 2)
-        apply_gain_rounded(last, final)
-        join_pairs(nc.scalar.copy, last, final - 1)
-        turn_pairs(last, final)
-        apply_gain(nc.vector, last, final, 0, WIDTH)
-        store_y(last, final)
-        join_pairs(nc.scalar.copy, last, final)
+                join_pairs(1, ct - 2)
+        apply_gain_rounded(1, final)
+        join_pairs(1, final - 1)
+        turn_pairs(1, final)
+        apply_gain(1, final)
+        join_pairs(1, final)
         quantize_y(0, 0, C_TILES)
-        store_codes(0, 0, CLUSTERS)
-        quantize_y(last, 0, 2)
-        store_codes(last, 0, 2 * P)
-        quantize_y(last, 2, 2)
-        store_codes(last, 2 * P, CLUSTERS)
-        store_scales()
+        quantize_y(1, 0, C_TILES // 2)
+        quantize_y(1, C_TILES // 2, C_TILES // 2)
+
+        for q in range(P // QUADRANT):
+            queue = nc.scalar if q % 2 == 0 else nc.sync
+            queue.dma_start(
+                out=out_2[:, SCALE_ROWS * q:SCALE_ROWS * (q + 1), :].bitcast(I32),
+                in_=y_scales[QUADRANT * q:QUADRANT * q + SCALE_ROWS * HALVES, :].bitcast(I32),
+            )

from contextlib import ExitStack

import concourse.mybir as mybir
from concourse.masks import make_identity

NODES, CLUSTERS, FEATS = 4096, 512, 1024
FLOPS = 2 * NODES * CLUSTERS * FEATS

F32 = mybir.dt.float32
BF16 = mybir.dt.bfloat16
I32 = mybir.dt.int32
U32 = mybir.dt.uint32
U8 = mybir.dt.uint8
FP8X4 = mybir.dt.float8_e4m3fn_x4
ALU = mybir.AluOpType

P = 128
PACK = 4
K_PASS = P * PACK
PASSES = NODES // K_PASS
WIDTH = 512
HALVES = FEATS // WIDTH
C_TILES = CLUSTERS // P
QUADRANT = 32
SCALE_ROWS = 4

RUN = 4
WHOLE_PASSES = 4
assert PASSES - WHOLE_PASSES == C_TILES
SCALAR_COLS_EARLY = 256
SCALAR_COLS_LATE = 456
SCALAR_COLS_END = 424

SIZE_ROW = QUADRANT - (CLUSTERS + 2 * FEATS) // P
SHIFT_ROW = SIZE_ROW + CLUSTERS // P
GAIN_ROW = SHIFT_ROW + FEATS // P


def tile_cluster_mean_pool_g1_kernel(tc, assign, x, sizes, shift, gain, out_0, out_1, out_2):
    nc = tc.nc

    with ExitStack() as ctx:
        keep = ctx.enter_context(tc.tile_pool(name="keep", bufs=1))
        stream = ctx.enter_context(tc.tile_pool(name="stream", bufs=4))
        psum = ctx.enter_context(tc.psum_pool(name="psum", bufs=1))
        ctx.enter_context(tc.manual_schedule())

        def bank(index, shape, dtype):
            return psum.tile(shape, dtype, name="bank%d" % index, tag="bank%d" % index)

        chunks = []
        for i in range(PASSES):
            chunks.append(("assign", i, 0))
            chunks.append(("x", i, 0))
            if i < WHOLE_PASSES:
                chunks.append(("x", i, 1))
        early_chunks = len(chunks)
        for i in range(WHOLE_PASSES, PASSES):
            chunks.append(("x", i, 1))

        def scalar_cols(n):
            if n <= early_chunks:
                return SCALAR_COLS_EARLY
            if n < len(chunks) - 1:
                return SCALAR_COLS_LATE
            return SCALAR_COLS_END

        rows = keep.tile([P, P], BF16, name="rows")
        nc.sync.dma_start(out=rows[SIZE_ROW:SHIFT_ROW, :], in_=sizes.rearrange("(j p) -> j p", p=P))
        nc.sync.dma_start(out=rows[SHIFT_ROW:GAIN_ROW, :], in_=shift.rearrange("(j p) -> j p", p=P))
        nc.sync.dma_start(out=rows[GAIN_ROW:QUADRANT, :], in_=gain.rearrange("(j p) -> j p", p=P))
        for lo, hi in ((0, SIZE_ROW), (QUADRANT, 2 * QUADRANT), (2 * QUADRANT, P)):
            nc.gpsimd.memset(rows[lo:hi, :], 0.0)
        ident_bf16 = keep.tile([P, P], BF16, name="ident_bf16")
        ident_f32 = keep.tile([P, P], F32, name="ident_f32")
        make_identity(nc, ident_bf16[:])
        make_identity(nc, ident_f32[:])

        raw = {}
        for chunk in chunks:
            kind, i, half = chunk
            if chunk not in raw:
                source = assign if kind == "assign" else x
                count = HALVES if kind == "x" and i < WHOLE_PASSES else 1
                block = source[i * K_PASS:(i + 1) * K_PASS, half * WIDTH:(half + count) * WIDTH]
                loaded = keep.tile([P, PACK, count * WIDTH], BF16, name="raw_%s%d_%d" % chunk)
                nc.sync.dma_start(out=loaded[:], in_=block.rearrange("(p t) w -> p t w", t=PACK))
                for k in range(count):
                    raw[kind, i, half + k] = loaded[:, :, k * WIDTH:(k + 1) * WIDTH]

        grouped = {}
        codes = {}
        scales = {}
        acc = {}

        def interleave(n):
            cut = scalar_cols(n)
            grouped[n] = stream.tile([P, WIDTH, PACK], BF16, name="grouped", align_bytes=64)
            for copy, lo, hi in ((nc.scalar.copy, 0, cut), (nc.vector.tensor_copy, cut, WIDTH)):
                copy(
                    out=grouped[n][:, lo:hi, :].rearrange("p (c i) t -> p c t i", i=RUN),
                    in_=raw[chunks[n]][:, :, lo:hi].rearrange("p t (c i) -> p c t i", i=RUN),
                )

        def quantize_and_multiply(n):
            kind, i, half = chunks[n]
            codes[chunks[n]] = keep.tile([P, WIDTH], U32, name="codes%d" % n, align_bytes=64)
            scales[chunks[n]] = keep.tile([P, WIDTH], U8, name="scales%d" % n, align_bytes=64)
            nc.vector.quantize_mx(
                out=codes[chunks[n]][:].bitcast(FP8X4),
                scales=scales[chunks[n]][:],
                in_=grouped[n][:].rearrange("p w t -> p (w t)"),
            )
            if kind == "x":
                for ct in range(C_TILES):
                    if i == 0:
                        acc[half, ct] = bank(half * C_TILES + ct, [P, WIDTH], F32)
                    cols = slice(ct * P, (ct + 1) * P)
                    nc.tensor.matmul_mx(
                        out=acc[half, ct][:],
                        lhsT=codes["assign", i, 0][:, cols].bitcast(FP8X4),
                        lhsT_scale=scales["assign", i, 0][:, cols],
                        rhs=codes["x", i, half][:].bitcast(FP8X4),
                        rhs_scale=scales["x", i, half][:],
                        start=(i == 0),
                        stop=(i == PASSES - 1),
                    )

        columns = keep.tile([P, QUADRANT], BF16, name="columns")
        inv_size = keep.tile([P, C_TILES], F32, name="inv_size")
        shift_all = keep.tile([P, FEATS], BF16, name="shift_all")
        gain_all = keep.tile([P, FEATS], BF16, name="gain_all")

        def spread(index, first_row):
            copies = bank(index, [P, FEATS], BF16)
            for m in range(FEATS // P):
                column = columns[:, first_row + m:first_row + m + 1]
                nc.tensor.transpose(copies[:, m * P:(m + 1) * P], column.to_broadcast([P, P]), ident_bf16[:])
            return copies

        y = {}
        y_pairs = {}
        turned_pairs = {}
        y_grouped = [
            keep.tile([P, CLUSTERS * PACK], BF16, name="y_grouped%d" % half, align_bytes=64) for half in range(HALVES)
        ]
        y_codes = [keep.tile([P, CLUSTERS], U32, name="y_codes%d" % half, align_bytes=64) for half in range(HALVES)]
        y_scales = keep.tile([P, CLUSTERS], U8, name="y_scales", align_bytes=64)

        def pool_and_shift(half, ct):
            y[half, ct] = keep.tile([P, WIDTH], F32, name="y%d_%d" % (half, ct))
            nc.vector.scalar_tensor_tensor(
                out=y[half, ct][:],
                in0=acc[half, ct][:],
                scalar=inv_size[:, ct:ct + 1],
                in1=shift_all[:, half * WIDTH:(half + 1) * WIDTH],
                op0=ALU.mult,
                op1=ALU.add,
            )

        def apply_gain(half, ct):
            nc.vector.tensor_tensor(
                out=y[half, ct][:],
                in0=y[half, ct][:],
                in1=gain_all[:, half * WIDTH:(half + 1) * WIDTH],
                op=ALU.mult,
            )
            nc.sync.dma_start(out=out_0[ct * P:(ct + 1) * P, half * WIDTH:(half + 1) * WIDTH], in_=y[half, ct][:])

        def by_pairs(ap):
            return ap.rearrange("c (p u e) -> c u p e", u=2, e=2)

        def round_y(half, ct):
            y_pairs[half, ct] = stream.tile([P, 2, P, 2], BF16, name="y_pairs")
            nc.scalar.copy(out=y_pairs[half, ct][:], in_=by_pairs(y[half, ct][:]))

        def apply_gain_rounded(half, ct):
            y_pairs[half, ct] = stream.tile([P, 2, P, 2], BF16, name="y_pairs")
            nc.vector.tensor_tensor(
                out=y_pairs[half, ct][:],
                in0=by_pairs(y[half, ct][:]),
                in1=by_pairs(gain_all[:, half * WIDTH:(half + 1) * WIDTH]),
                op=ALU.mult,
            )

        def turn_pairs(half, ct):
            turned_pairs[half, ct] = bank(ct, [P, 2, P], F32)
            pairs = y_pairs[half, ct][:].rearrange("c u p e -> c (u p e)").bitcast(F32)
            for u in range(2):
                nc.tensor.transpose(turned_pairs[half, ct][:, u, :], pairs[:, u * P:(u + 1) * P], ident_f32[:])

        def join_pairs(half, ct):
            target = y_grouped[half][:, ct * P * PACK:(ct + 1) * P * PACK]
            nc.scalar.copy(
                out=target.bitcast(F32).rearrange("p (c u) -> p c u", u=2),
                in_=turned_pairs[half, ct][:].rearrange("p u c -> p c u"),
            )

        def quantize_y(half, first, count):
            cols = slice(first * P, (first + count) * P)
            nc.vector.quantize_mx(
                out=y_codes[half][:, cols].bitcast(FP8X4),
                scales=y_scales[SCALE_ROWS * half:P, cols],
                in_=y_grouped[half][:, first * P * PACK:(first + count) * P * PACK],
            )
            nc.sync.dma_start(
                out=out_1[half, :, cols, :].rearrange("p m t -> p (m t)").bitcast(I32),
                in_=y_codes[half][:, cols].bitcast(I32),
            )

        turned_rows = bank(C_TILES, [P, P], BF16)
        nc.tensor.transpose(turned_rows[:], rows[:], ident_bf16[:])
        nc.vector.tensor_copy(out=columns[:], in_=turned_rows[:, 0:QUADRANT])
        shift_copies = spread(C_TILES + 1, SHIFT_ROW)
        gain_copies = spread(C_TILES + 2, GAIN_ROW)

        final = C_TILES - 1
        for n in range(len(chunks)):
            interleave(n)
            late = n - early_chunks
            if late == final:
                round_y(0, 0)
            if n >= 1:
                quantize_and_multiply(n - 1)
            if late == 1:
                pool_and_shift(0, 0)
            if late >= 1:
                pool_and_shift(0, late)
                apply_gain(0, late - 1)
            if n == 0:
                nc.vector.reciprocal(out=inv_size[:], in_=columns[:, SIZE_ROW:SHIFT_ROW])
                nc.vector.tensor_copy(out=shift_all[:], in_=shift_copies[:])
                nc.vector.tensor_copy(out=gain_all[:], in_=gain_copies[:])
        quantize_and_multiply(len(chunks) - 1)

        apply_gain(0, final)
        turn_pairs(0, 0)
        for ct in range(1, C_TILES):
            round_y(0, ct)
            turn_pairs(0, ct)
        for ct in range(C_TILES):
            join_pairs(0, ct)

        for ct in range(C_TILES):
            pool_and_shift(1, ct)
            if ct >= 1:
                apply_gain(1, ct - 1)
                round_y(1, ct - 1)
                turn_pairs(1, ct - 1)
            if ct >= 2:
                join_pairs(1, ct - 2)
        apply_gain_rounded(1, final)
        join_pairs(1, final - 1)
        turn_pairs(1, final)
        apply_gain(1, final)
        join_pairs(1, final)
        quantize_y(0, 0, C_TILES)
        quantize_y(1, 0, C_TILES // 2)
        quantize_y(1, C_TILES // 2, C_TILES // 2)

        for q in range(P // QUADRANT):
            queue = nc.scalar if q % 2 == 0 else nc.sync
            queue.dma_start(
                out=out_2[:, SCALE_ROWS * q:SCALE_ROWS * (q + 1), :].bitcast(I32),
                in_=y_scales[QUADRANT * q:QUADRANT * q + SCALE_ROWS * HALVES, :].bitcast(I32),
            )
